import numpy as np
import ml_dtypes


def mxq(x, axis, fmt="e4m3"):
    dtype, down = {"e4m3": (ml_dtypes.float8_e4m3fn, 7), "e5m2": (ml_dtypes.float8_e5m2, 14)}[fmt]
    v = np.moveaxis(np.asarray(x, np.float32).astype(ml_dtypes.bfloat16).astype(np.float64), axis, -1)
    blocks = v.reshape(v.shape[:-1] + (-1, 32))
    amax = np.abs(blocks).max(-1, keepdims=True)
    byte = np.maximum(np.where(amax > 0, np.frexp(amax)[1] - 1 + 127, 0) - down, 1)
    scale = np.exp2(byte - 127.0)
    codes = (blocks / scale).astype(np.float32).astype(dtype).astype(np.float64)
    return np.moveaxis((codes * scale).reshape(v.shape), -1, axis)


WIDE = False


def mx_kscale(k):
    if not WIDE:
        return np.ones(k)
    levels = np.array([10, -10, 5, -5, 0])
    if k % 512:
        return np.exp2(np.random.permutation(np.resize(levels, k // 32))).repeat(32)
    a = np.empty((k // 512, 16))
    for p in range(k // 512):
        a[p, :8] = np.random.permutation(np.resize(levels, 8))
        for g in range(8):
            far = levels[np.abs(levels - a[p, g]) >= 10]
            a[p, g + 8] = far[np.random.randint(len(far))]
    return np.exp2(a.ravel()).repeat(32)


def f64(x):
    return np.asarray(x).astype(np.float64)


def striped(idx):
    return np.tile(idx.reshape(-1, 16).T, (8, 1)).astype(np.uint16)


def unstriped(offs):
    return offs[:16].T.reshape(-1).astype(np.int64)


E2M1 = np.array([0.0, 0.5, 1.0, 1.5, 2.0, 3.0, 4.0, 6.0, -0.0, -0.5, -1.0, -1.5, -2.0, -3.0, -4.0, -6.0])


def pack_weight(w, fmt):
    k, n = w.shape
    w = f64(np.asarray(w, np.float32).astype(ml_dtypes.bfloat16)).reshape(k // 32, 32, n)
    amax = np.abs(w).max(1)
    if fmt == "e4m3":
        byte = np.frexp(amax)[1] - 1 + 127 - 7
    else:
        mant, ex = np.frexp(amax / 6.0)
        byte = np.where(mant > 0.5, ex, ex - 1) + 127
    byte = np.clip(np.where(amax > 0, byte, 1), 1, 254)
    scaled = (w * np.exp2(127.0 - byte)[:, None, :]).reshape(k, n).astype(np.float32)
    by_word = np.ascontiguousarray(scaled.reshape(k // 512, 128, 4, n).transpose(0, 1, 3, 2))
    if fmt == "e4m3":
        words = by_word.astype(ml_dtypes.float8_e4m3fn).view(np.uint8)
    else:
        c = by_word.astype(ml_dtypes.float4_e2m1fn).view(np.uint8) & 0xF
        words = (c[..., 0::2] | (c[..., 1::2] << 4)).reshape(k // 512, 128, 2 * n)
    return np.ascontiguousarray(words), np.ascontiguousarray(byte.astype(np.uint8).reshape(k // 512, 16, n))


def unpack_weight(words, scales, fmt):
    g, _, n = scales.shape
    words = np.ascontiguousarray(words).reshape(g, 128, n, -1)
    if fmt == "e4m3":
        vals = words.view(ml_dtypes.float8_e4m3fn).astype(np.float64)
    else:
        nib = np.empty((g, 128, n, 4), np.uint8)
        nib[..., 0::2] = words & 0xF
        nib[..., 1::2] = words >> 4
        vals = E2M1[nib]
    vals = vals * np.repeat(np.exp2(scales.astype(np.float64) - 127.0), 8, axis=1)[..., None]
    return vals.transpose(0, 1, 3, 2).reshape(g * 512, n)


def gelu(v):
    return 0.5 * v * (1.0 + np.tanh(np.sqrt(2.0 / np.pi) * (v + 0.044715 * v**3)))


def striped8(idx):
    return np.concatenate([v.reshape(-1, 16).T for v in idx]).astype(np.uint16)


def unstriped8(offs):
    return np.stack([offs[16 * g:16 * g + 16].T.reshape(-1) for g in range(8)]).astype(np.int64)


def heads(h, wgt, idx8):
    r = np.arange(h.shape[0])
    return wgt[r // 4 % 128] * h[r[:, None], idx8[r % 512 // 64]]


K, T, S, H, T2, P, N = 1024, 2048, 512, 1024, 1024, 512, 512

def setup_inputs():
    n = np.random.standard_normal
    s, u = mx_kscale(K)[:, None], mx_kscale(H)[:, None]
    tab_words, tab_scales = pack_weight(n((K, T)) * s, "e4m3")
    w1 = 0.8 * n((K, H)) * u.T / (s * np.sqrt(K))
    w4_words, w4_scales = pack_weight(0.8 * n((K, H)) * u.T / (s * np.sqrt(K)), "e2m1")
    w2 = n((H, N)) / (u * np.sqrt(H))
    strips = np.stack([np.random.permutation(T2)[:P] for _ in range(8)])
    return {
        "tab_words": tab_words, "tab_scales": tab_scales,
        "offs": striped(np.random.permutation(T)[:S]),
        "offs2": striped(np.random.permutation(T2)[:S]),
        "offs3": striped8(strips),
        "w1": w1.astype(np.float32),
        "w4_words": w4_words, "w4_scales": w4_scales,
        "gain": np.random.uniform(0.6, 1.2, H).astype(np.float32),
        "wgs": np.exp(0.3 * n((128, S))).astype(np.float32),
        "page0": (0.8 * n((H, T2)) * u).astype(np.float32),
        "wgt": np.repeat(np.random.uniform(0.5, 2.0, (8, P)), 16, axis=0).astype(np.float32),
        "pitch": (np.random.uniform(0.07, 0.13, H) / u[:, 0]).astype(np.float32),
        "slope": np.random.uniform(-1.4, 1.4, (H, P)).astype(np.float32),
        "w2": w2.astype(np.float32),
    }

def reference(tab_words, tab_scales, offs, offs2, offs3, w1, w4_words, w4_scales, gain, wgs, page0, wgt, pitch, slope, w2):
    v = unpack_weight(tab_words, tab_scales, "e4m3")[:, unstriped(offs)]
    w4 = unpack_weight(w4_words, w4_scales, "e2m1")
    a = mxq(f64(w1), 0, "e4m3").T @ v
    b = w4.T @ v
    h = np.maximum(a, f64(gain)[:, None] * b)
    page = f64(page0).copy()
    page[:, unstriped(offs2)] = np.tile(f64(wgs), (H // 128, 1)) * h
    x = heads(page, f64(wgt), unstriped8(offs3))
    z = x * np.cos(f64(pitch)[:, None] * x + f64(slope))
    return mxq(f64(w2), 0, "e4m3").T @ mxq(z, 0, "e4m3")

@@ -1,0 +1,261 @@
+import math
+from contextlib import ExitStack
+
+import concourse.mybir as mybir
+from concourse.masks import make_identity
+
+K, T, S, H, T2, M, N = 1024, 2048, 512, 1024, 1024, 512, 512
+FLOPS = 2 * (2 * K * H * S + H * N * M)
+
+F32, BF16 = mybir.dt.float32, mybir.dt.bfloat16
+I32, U32, U16, U8 = mybir.dt.int32, mybir.dt.uint32, mybir.dt.uint16, mybir.dt.uint8
+E4M3, E2M1 = mybir.dt.float8_e4m3fn_x4, mybir.dt.float4_e2m1fn_x4
+ALU, ACT = mybir.AluOpType, mybir.ActivationFunctionType
+
+P = 128
+PACK = 4
+KP = P * PACK
+TWO_PI = 2.0 * math.pi
+
+
+def tile_list_blade_load_cells_kernel(tc, tab_words, tab_scales, offs, offs2, offs3, w1, w4_words, w4_scales,
+                                                gain, wgs, page0, wgt, pitch, slope, w2, out):
+    nc = tc.nc
+    with ExitStack() as ctx:
+        held = ctx.enter_context(tc.tile_pool(name="held", bufs=1))
+        raws = ctx.enter_context(tc.tile_pool(name="raws", bufs=4))
+        ring = ctx.enter_context(tc.tile_pool(name="ring", bufs=2))
+        psum = ctx.enter_context(tc.psum_pool(name="psum", bufs=2))
+
+        def keep(shape, dtype, name):
+            return held.tile(shape, dtype, name=name, align_bytes=64)
+
+        tab_sc = keep([P, 2 * T], U8, "tab_sc")
+        w4_sc_raw = keep([P, 2 * H], U8, "w4_sc_raw")
+        nc.vector.memset(w4_sc_raw[:].bitcast(I32), 0)
+        nc.vector.memset(tab_sc[:].bitcast(I32), 0)
+
+        def load_scales(queue, tile, rows):
+            for q in range(4):
+                queue.dma_start(
+                    out=tile[32 * q:32 * q + 4, :].bitcast(I32).rearrange("r (a c) -> r a c", a=2),
+                    in_=rows[:, 4 * q:4 * q + 4, :].bitcast(I32).rearrange("a r c -> r a c"))
+
+        gain_sb = keep([P, 2, PACK], F32, "gain_sb")
+        pitch_sb = keep([P, 2, PACK], F32, "pitch_sb")
+        ident = keep([P, P], F32, "ident")
+        make_identity(nc, ident[:])
+        half_pi = keep([P, 1], F32, "half_pi")
+        nc.vector.memset(half_pi[:], 1.0)
+        nc.vector.tensor_scalar(half_pi[:], half_pi[:], math.pi / 2, None, ALU.mult)
+
+        list1 = held.tile([P, S // 16], U16, name="list1")
+        list2 = held.tile([P, S // 16], U16, name="list2")
+        list3 = held.tile([P, M // 16], U16, name="list3")
+        w4_raw = keep([P, 2, H // 2], I32, "w4_raw")
+        tab = [keep([P, T], I32, "tab%d" % a) for a in range(2)]
+        pages = [keep([P, T2], F32, "page%d" % s) for s in range(8)]
+        slopes = [keep([P, M], F32, "slope%d" % s) for s in range(8)]
+        wgs_sb = [keep([P, S], F32, "wgs%d" % i) for i in range(PACK)]
+        wgt_sb = keep([P, M], F32, "wgt_sb")
+        page_rows = page0.rearrange("(b p i) c -> b i p c", b=2, i=PACK)
+        slope_rows = slope.rearrange("(b p i) c -> b i p c", b=2, i=PACK)
+        wgs_rows = wgs.rearrange("(q i) j -> q i j", i=PACK)
+
+        def load_rows(w, a, cols):
+            raw = raws.tile([P, PACK, 512], F32, name="raw")
+            nc.sync.dma_start(out=raw[:], in_=w[KP * a:KP * (a + 1), cols].rearrange("(p j) c -> p j c", j=PACK))
+            return raw
+
+        def load_wgs(i):
+            for q in range(4):
+                nc.sync.dma_start(out=wgs_sb[i][32 * q:32 * q + 32, :], in_=wgs_rows[:, i, :])
+
+        def load_page(s):
+            nc.sync.dma_start(out=pages[s][:], in_=page_rows[s // 4, s % 4])
+
+        def load_slope(s):
+            nc.sync.dma_start(out=slopes[s][:], in_=slope_rows[s // 4, s % 4])
+
+        def load_table(a):
+            nc.sync.dma_start(out=tab[a][:], in_=tab_words[a].rearrange("p t i -> p (t i)").bitcast(I32))
+
+        nc.sync.dma_start(out=w4_raw[:], in_=w4_words.bitcast(I32).rearrange("a p c -> p a c"))
+        load_scales(nc.sync, w4_sc_raw, w4_scales)
+        nc.sync.dma_start(list1[:], offs)
+        load_table(0)
+        load_scales(nc.sync, tab_sc, tab_scales)
+        load_table(1)
+        w1_raw = {}
+        for a in range(2):
+            w1_raw[a, 0] = load_rows(w1, a, slice(0, 512))
+        nc.sync.dma_start(out=gain_sb[:], in_=gain.rearrange("(b p i) -> p b i", b=2, i=PACK))
+        nc.sync.dma_start(list2[:], offs2)
+        load_page(0)
+        load_wgs(0)
+        nc.sync.dma_start(list3[:], offs3)
+        nc.sync.dma_start(out=wgt_sb[:], in_=wgt)
+        nc.sync.dma_start(out=pitch_sb[:], in_=pitch.rearrange("(b p i) -> p b i", b=2, i=PACK))
+        load_slope(0)
+        for s in range(1, 3):
+            load_page(s)
+            load_wgs(s)
+            load_slope(s)
+        for a in range(2):
+            w1_raw[a, 1] = load_rows(w1, a, slice(512, 1024))
+        load_wgs(3)
+        for s in range(3, 8):
+            load_page(s)
+            load_slope(s)
+        w2_raw = [load_rows(w2, b, slice(0, N)) for b in range(2)]
+
+        w4_codes = keep([P, 2 * 2 * H], U8, "w4_codes")
+        w4_sc = keep([P, 2 * H], U8, "w4_sc")
+        nc.vector.tensor_copy(
+            w4_codes[:].bitcast(U16).rearrange("p (g i m) -> p g i m", g=4, i=PACK),
+            w4_raw[:].rearrange("p a c -> p (a c)").bitcast(U16).rearrange("p (g m i) -> p g i m", g=4, i=PACK))
+        nc.vector.tensor_copy(
+            w4_sc[:].rearrange("p (g i m) -> p g i m", g=4, i=PACK),
+            w4_sc_raw[:].rearrange("p (g m i) -> p g i m", g=4, i=PACK))
+
+        v_codes = [keep([P, S], U32, "v_codes%d" % a) for a in range(2)]
+        v_sc = [keep([P, S], U8, "v_sc%d" % a) for a in range(2)]
+        for a in range(2):
+            nc.vector.tensor_copy(v_sc[a][:], tab_sc[:, T * a:T * (a + 1)].indirect(list1[:]))
+            nc.vector.tensor_copy(v_codes[a][:], tab[a][:].bitcast(U32).indirect(list1[:]))
+
+        w1_codes, w1_sc = {}, {}
+
+        def quantise_w1(a, b, u):
+            grouped = ring.tile([P, 2, P, PACK], BF16, name="w1_bf", align_bytes=64)
+            dst = grouped[:].rearrange("p i m j -> p m j i")
+            src = w1_raw[a, b][:].rearrange("p j (m i) -> p m j i", i=PACK)[:, :, :, 2 * u:2 * u + 2]
+            if (a, b, u) == (1, 0, 0):
+                nc.vector.tensor_copy(dst, src)
+            else:
+                nc.scalar.copy(dst, src)
+            w1_codes[a, b, u] = keep([P, 2 * P], U32, "w1_codes%d%d%d" % (a, b, u))
+            w1_sc[a, b, u] = keep([P, 2 * P], U8, "w1_sc%d%d%d" % (a, b, u))
+            nc.vector.quantize_mx(out=w1_codes[a, b, u][:].bitcast(E4M3), scales=w1_sc[a, b, u][:],
+                                  in_=grouped[:].rearrange("p i m j -> p (i m j)"))
+
+        w2_codes = [keep([P, N], U32, "w2_codes%d" % b) for b in range(2)]
+        w2_sc = [keep([P, N], U8, "w2_sc%d" % b) for b in range(2)]
+
+        def quantise_w2(b):
+            grouped = keep([P, N, PACK], BF16, "w2_bf%d" % b)
+            nc.scalar.copy(grouped[:].rearrange("p (c e) j -> p c j e", e=2),
+                           w2_raw[b][:].rearrange("p j (c e) -> p c j e", e=2))
+            nc.vector.quantize_mx(out=w2_codes[b][:].bitcast(E4M3), scales=w2_sc[b][:],
+                                  in_=grouped[:].rearrange("p c j -> p (c j)"))
+
+        x = [keep([P, PACK, M], F32, "x%d" % b) for b in range(2)]
+        cosine = [keep([P, PACK, M], F32, "cosine%d" % b) for b in range(2)]
+        z_codes = [keep([P, M], U32, "z_codes%d" % b) for b in range(2)]
+        z_sc = [keep([P, M], U8, "z_sc%d" % b) for b in range(2)]
+        h_of = {}
+
+        def features(s):
+            b, i = divmod(s, PACK)
+            u, e = divmod(i, 2)
+            first = psum.tile([P, S], F32, name="first")
+            second = psum.tile([P, S], F32, name="second")
+            for a in range(2):
+                col = (2 * a + b) * KP + i * P
+                nc.tensor.matmul_mx(out=second[:], lhsT=w4_codes[:, 2 * col:2 * (col + P)].bitcast(E2M1),
+                                    lhsT_scale=w4_sc[:, col:col + P], rhs=v_codes[a][:].bitcast(E4M3),
+                                    rhs_scale=v_sc[a][:], start=(a == 0), stop=(a == 1))
+            for a in range(2):
+                nc.tensor.matmul_mx(out=first[:], lhsT=w1_codes[a, b, u][:, e * P:(e + 1) * P].bitcast(E4M3),
+                                    lhsT_scale=w1_sc[a, b, u][:, e * P:(e + 1) * P], rhs=v_codes[a][:].bitcast(E4M3),
+                                    rhs_scale=v_sc[a][:], start=(a == 0), stop=(a == 1))
+            gained = ring.tile([P, S], F32, name="gained")
+            nc.scalar.activation(gained[:], second[:], ACT.Copy, scale=gain_sb[:, b, i:i + 1])
+            h_of[s] = ring.tile([P, S], F32, name="h", bufs=3, align_bytes=64)
+            nc.vector.tensor_tensor(h_of[s][:], first[:], gained[:], ALU.max)
+
+        def put(s):
+            i = s % PACK
+            nc.vector.tensor_tensor(pages[s][:].indirect(list2[:]), h_of[s][:], wgs_sb[i][:], ALU.mult)
+
+        def pick(s, cols):
+            b, i = divmod(s, PACK)
+            nc.vector.tensor_tensor(x[b][:, i, cols], pages[s][:].indirect(list3[:, cols.start // 16:cols.stop // 16]),
+                                    wgt_sb[:, cols], ALU.mult)
+
+        def add_turned(bank, one, other):
+            for n, src in enumerate((one, other)):
+                for c in range(4):
+                    nc.tensor.matmul(bank[:, c * P:(c + 1) * P], lhsT=src[:, c * P:(c + 1) * P], rhs=ident[:],
+                                     is_transpose=True, start=(n == 0 and c == 0), stop=(n == 1 and c == 3))
+
+        def cos_by_tensor(s):
+            b, i = divmod(s, PACK)
+            pitched = ring.tile([P, M], F32, name="pitched")
+            nc.scalar.activation(pitched[:], x[b][:, i, :], ACT.Copy, scale=pitch_sb[:, b, i:i + 1])
+            theta = psum.tile([P, M], F32, name="theta")
+            add_turned(theta, slopes[s], pitched)
+            size = ring.tile([P, M], F32, name="size")
+            nc.scalar.activation(size[:], theta[:], ACT.Abs)
+            turns = ring.tile([P, M], U32, name="turns")
+            nc.scalar.activation(turns[:], size[:], ACT.Copy, scale=1.0 / TWO_PI, bias=-0.25)
+            whole = ring.tile([P, M], F32, name="whole")
+            nc.scalar.activation(whole[:], turns[:], ACT.Copy, scale=-TWO_PI)
+            rest = psum.tile([P, M], F32, name="rest")
+            add_turned(rest, size, whole)
+            nc.scalar.activation(cosine[b][:, i, :], rest[:], ACT.Sin, scale=-1.0, bias=half_pi[:])
+
+        def cos_by_vector(s, cols):
+            b, i = divmod(s, PACK)
+            width = cols.stop - cols.start
+            theta = ring.tile([P, width], F32, name="pitched")
+            nc.vector.scalar_tensor_tensor(theta[:], x[b][:, i, cols], pitch_sb[:, b, i:i + 1], slopes[s][:, cols],
+                                           ALU.mult, ALU.add)
+            size = ring.tile([P, width], F32, name="size")
+            nc.scalar.activation(size[:], theta[:], ACT.Abs)
+            turns = ring.tile([P, width], U32, name="turns")
+            nc.scalar.activation(turns[:], size[:], ACT.Copy, scale=1.0 / TWO_PI, bias=-0.25)
+            rest = ring.tile([P, width], F32, name="whole")
+            nc.vector.scalar_tensor_tensor(rest[:], turns[:].bitcast(I32), TWO_PI, size[:], ALU.mult, ALU.subtract)
+            nc.scalar.activation(cosine[b][:, i, cols], rest[:], ACT.Sin, bias=half_pi[:])
+
+        def quantise_z(b, cols, room):
+            z = room[:].bitcast(BF16)
+            nc.vector.tensor_tensor(z.rearrange("p (c e i) -> p c i e", e=2, i=PACK),
+                                    x[b][:, :, cols].rearrange("p i (c e) -> p c i e", e=2),
+                                    cosine[b][:, :, cols].rearrange("p i (c e) -> p c i e", e=2), ALU.mult)
+            nc.vector.quantize_mx(out=z_codes[b][:, cols].bitcast(E4M3), scales=z_sc[b][:, cols], in_=z)
+
+        halves = (slice(0, M // 2), slice(M // 2, M))
+        for s in range(8):
+            if s % 2 == 0:
+                for a in range(2):
+                    quantise_w1(a, s // 4, s % 4 // 2)
+            features(s)
+            put(s)
+            if s in (5, 6):
+                quantise_z(0, halves[s - 5], h_of[s])
+                quantise_w2(s - 5)
+            if s < 7:
+                pick(s, slice(0, M))
+                cos_by_tensor(s)
+        for cols in halves:
+            pick(7, cols)
+            cos_by_vector(7, cols)
+
+        for cols, banks in zip(halves, (("first", "second"), ("theta", "rest"))):
+            accs = [psum.tile([P, M // 2], F32, name=banks[n % 2]) for n in range(N // P)]
+            room = ring.tile([P, S], F32, name="h", bufs=3, align_bytes=64)
+            quantise_z(1, cols, room)
+            for n in range(N // P):
+                for b in range(2):
+                    nc.tensor.matmul_mx(out=accs[n][:], lhsT=w2_codes[b][:, n * P:(n + 1) * P].bitcast(E4M3),
+                                        lhsT_scale=w2_sc[b][:, n * P:(n + 1) * P],
+                                        rhs=z_codes[b][:, cols].bitcast(E4M3),
+                                        rhs_scale=z_sc[b][:, cols], start=(b == 0), stop=(b == 1))
+                result = keep([P, M // 2], F32, "result%d%d" % (n, cols.start))
+                if cols.start == 0 or n % 2 == 0:
+                    nc.scalar.copy(result[:], accs[n][:])
+                else:
+                    nc.vector.tensor_copy(result[:], accs[n][:])
+                nc.sync.dma_start(out=out[n * P:(n + 1) * P, cols], in_=result[:])

@@ -16,6 +16,10 @@ P = 128
 PACK = 4
 KP = P * PACK
 TWO_PI = 2.0 * math.pi
+T_OF = (3, 2, 3, 2, 3, 2, 3)
+F_OF = (0, 1, 0, 1, 2, 3, 0, 1)
+TH_OF = (2, 3, 0, 1, 2, 3, 0)
+H_OF = (0, 0, 1, 0, 1, 0, 1, 0)
 
 
 def tile_list_blade_load_cells_kernel(tc, tab_words, tab_scales, offs, offs2, offs3, w1, w4_words, w4_scales,
@@ -25,7 +29,7 @@ def tile_list_blade_load_cells_kernel(tc, tab_words, tab_scales, offs, offs2, of
         held = ctx.enter_context(tc.tile_pool(name="held", bufs=1))
         raws = ctx.enter_context(tc.tile_pool(name="raws", bufs=4))
         ring = ctx.enter_context(tc.tile_pool(name="ring", bufs=2))
-        psum = ctx.enter_context(tc.psum_pool(name="psum", bufs=2))
+        psum = ctx.enter_context(tc.psum_pool(name="psum", bufs=1))
 
         def keep(shape, dtype, name):
             return held.tile(shape, dtype, name=name, align_bytes=64)
@@ -56,7 +60,9 @@ def tile_list_blade_load_cells_kernel(tc, tab_words, tab_scales, offs, offs2, of
         tab = [keep([P, T], I32, "tab%d" % a) for a in range(2)]
         pages = [keep([P, T2], F32, "page%d" % s) for s in range(8)]
         slopes = [keep([P, M], F32, "slope%d" % s) for s in range(8)]
-        wgs_sb = [keep([P, S], F32, "wgs%d" % i) for i in range(PACK)]
+        wgs_first = keep([P, 1, S], F32, "wgs_first")
+        wgs_rest = keep([P, PACK - 1, S], F32, "wgs_rest")
+        wgs_sb = [wgs_first[:, 0, :]] + [wgs_rest[:, i, :] for i in range(PACK - 1)]
         wgt_sb = keep([P, M], F32, "wgt_sb")
         page_rows = page0.rearrange("(b p i) c -> b i p c", b=2, i=PACK)
         slope_rows = slope.rearrange("(b p i) c -> b i p c", b=2, i=PACK)
@@ -67,9 +73,9 @@ def tile_list_blade_load_cells_kernel(tc, tab_words, tab_scales, offs, offs2, of
             nc.sync.dma_start(out=raw[:], in_=w[KP * a:KP * (a + 1), cols].rearrange("(p j) c -> p j c", j=PACK))
             return raw
 
-        def load_wgs(i):
+        def load_wgs(tile, rows):
             for q in range(4):
-                nc.sync.dma_start(out=wgs_sb[i][32 * q:32 * q + 32, :], in_=wgs_rows[:, i, :])
+                nc.sync.dma_start(out=tile[32 * q:32 * q + 32], in_=wgs_rows[:, rows, :])
 
         def load_page(s):
             nc.sync.dma_start(out=pages[s][:], in_=page_rows[s // 4, s % 4])
@@ -92,22 +98,24 @@ def tile_list_blade_load_cells_kernel(tc, tab_words, tab_scales, offs, offs2, of
         nc.sync.dma_start(out=gain_sb[:], in_=gain.rearrange("(b p i) -> p b i", b=2, i=PACK))
         nc.sync.dma_start(list2[:], offs2)
         load_page(0)
-        load_wgs(0)
+        load_wgs(wgs_first, slice(0, 1))
         nc.sync.dma_start(list3[:], offs3)
         nc.sync.dma_start(out=wgt_sb[:], in_=wgt)
+        load_page(1)
+        load_wgs(wgs_rest, slice(1, PACK))
         nc.sync.dma_start(out=pitch_sb[:], in_=pitch.rearrange("(b p i) -> p b i", b=2, i=PACK))
-        load_slope(0)
-        for s in range(1, 3):
+        w2_raw = {}
+        for s in range(2, 6):
+            load_slope(s - 2)
+            if s < 4:
+                w1_raw[s - 2, 1] = load_rows(w1, s - 2, slice(512, 1024))
+            else:
+                w2_raw[s - 4] = load_rows(w2, s - 4, slice(0, N))
             load_page(s)
-            load_wgs(s)
-            load_slope(s)
-        for a in range(2):
-            w1_raw[a, 1] = load_rows(w1, a, slice(512, 1024))
-        load_wgs(3)
-        for s in range(3, 8):
+        for s in range(6, 8):
+            load_slope(2 * s - 8)
+            load_slope(2 * s - 7)
             load_page(s)
-            load_slope(s)
-        w2_raw = [load_rows(w2, b, slice(0, N)) for b in range(2)]
 
         w4_codes = keep([P, 2 * 2 * H], U8, "w4_codes")
         w4_sc = keep([P, 2 * H], U8, "w4_sc")
@@ -127,7 +135,7 @@ def tile_list_blade_load_cells_kernel(tc, tab_words, tab_scales, offs, offs2, of
         w1_codes, w1_sc = {}, {}
 
         def quantise_w1(a, b, u):
-            grouped = ring.tile([P, 2, P, PACK], BF16, name="w1_bf", align_bytes=64)
+            grouped = ring.tile([P, 2, P, PACK], BF16, name="w1_bf", bufs=4, align_bytes=64)
             dst = grouped[:].rearrange("p i m j -> p m j i")
             src = w1_raw[a, b][:].rearrange("p j (m i) -> p m j i", i=PACK)[:, :, :, 2 * u:2 * u + 2]
             if (a, b, u) == (1, 0, 0):
@@ -144,8 +152,9 @@ def tile_list_blade_load_cells_kernel(tc, tab_words, tab_scales, offs, offs2, of
 
         def quantise_w2(b):
             grouped = keep([P, N, PACK], BF16, "w2_bf%d" % b)
-            nc.scalar.copy(grouped[:].rearrange("p (c e) j -> p c j e", e=2),
-                           w2_raw[b][:].rearrange("p j (c e) -> p c j e", e=2))
+            for cols in (slice(0, N // 2), slice(N // 2, N)):
+                nc.scalar.copy(grouped[:, cols, :].rearrange("p (c e) j -> p c j e", e=2),
+                               w2_raw[b][:, :, cols].rearrange("p j (c e) -> p c j e", e=2))
             nc.vector.quantize_mx(out=w2_codes[b][:].bitcast(E4M3), scales=w2_sc[b][:],
                                   in_=grouped[:].rearrange("p c j -> p (c j)"))
 
@@ -153,30 +162,36 @@ def tile_list_blade_load_cells_kernel(tc, tab_words, tab_scales, offs, offs2, of
         cosine = [keep([P, PACK, M], F32, "cosine%d" % b) for b in range(2)]
         z_codes = [keep([P, M], U32, "z_codes%d" % b) for b in range(2)]
         z_sc = [keep([P, M], U8, "z_sc%d" % b) for b in range(2)]
-        h_of = {}
+        gained = {}
+        h = [keep([P, S], F32, "h%d" % e) for e in range(4)]
+        sizes = [keep([P, M], F32, "size%d" % e) for e in range(2)]
+        turn_banks = [psum.tile([P, M], F32, name="turn%d" % e) for e in range(4)]
+        rest_banks = [psum.tile([P, M], F32, name="rest%d" % e) for e in range(2)]
 
-        def features(s):
+        def gained_feature(s):
             b, i = divmod(s, PACK)
-            u, e = divmod(i, 2)
-            first = psum.tile([P, S], F32, name="first")
-            second = psum.tile([P, S], F32, name="second")
+            second = psum.tile([P, S], F32, name="second", bufs=2)
             for a in range(2):
                 col = (2 * a + b) * KP + i * P
                 nc.tensor.matmul_mx(out=second[:], lhsT=w4_codes[:, 2 * col:2 * (col + P)].bitcast(E2M1),
                                     lhsT_scale=w4_sc[:, col:col + P], rhs=v_codes[a][:].bitcast(E4M3),
                                     rhs_scale=v_sc[a][:], start=(a == 0), stop=(a == 1))
+            gained[s] = ring.tile([P, S], F32, name="gained")
+            nc.scalar.activation(gained[s][:], second[:], ACT.Copy, scale=gain_sb[:, b, i:i + 1])
+
+        def larger_feature(s):
+            b, i = divmod(s, PACK)
+            u, e = divmod(i, 2)
+            first = turn_banks[F_OF[s]]
             for a in range(2):
                 nc.tensor.matmul_mx(out=first[:], lhsT=w1_codes[a, b, u][:, e * P:(e + 1) * P].bitcast(E4M3),
                                     lhsT_scale=w1_sc[a, b, u][:, e * P:(e + 1) * P], rhs=v_codes[a][:].bitcast(E4M3),
                                     rhs_scale=v_sc[a][:], start=(a == 0), stop=(a == 1))
-            gained = ring.tile([P, S], F32, name="gained")
-            nc.scalar.activation(gained[:], second[:], ACT.Copy, scale=gain_sb[:, b, i:i + 1])
-            h_of[s] = ring.tile([P, S], F32, name="h", bufs=3, align_bytes=64)
-            nc.vector.tensor_tensor(h_of[s][:], first[:], gained[:], ALU.max)
+            nc.vector.tensor_tensor(h[H_OF[s]][:], first[:], gained[s][:], ALU.max)
 
         def put(s):
             i = s % PACK
-            nc.vector.tensor_tensor(pages[s][:].indirect(list2[:]), h_of[s][:], wgs_sb[i][:], ALU.mult)
+            nc.vector.tensor_tensor(pages[s][:].indirect(list2[:]), h[H_OF[s]][:], wgs_sb[i], ALU.mult)
 
         def pick(s, cols):
             b, i = divmod(s, PACK)
@@ -191,71 +206,90 @@ def tile_list_blade_load_cells_kernel(tc, tab_words, tab_scales, offs, offs2, of
 
         def cos_by_tensor(s):
             b, i = divmod(s, PACK)
-            pitched = ring.tile([P, M], F32, name="pitched")
-            nc.scalar.activation(pitched[:], x[b][:, i, :], ACT.Copy, scale=pitch_sb[:, b, i:i + 1])
-            theta = psum.tile([P, M], F32, name="theta")
-            add_turned(theta, slopes[s], pitched)
-            size = ring.tile([P, M], F32, name="size")
+            theta, rest, size = turn_banks[TH_OF[s]], rest_banks[s % 2], sizes[s % 2]
+            turns = h[T_OF[s]][:].bitcast(U32)
+            nc.scalar.activation(size[:], x[b][:, i, :], ACT.Copy, scale=pitch_sb[:, b, i:i + 1])
+            add_turned(theta, slopes[s], size)
             nc.scalar.activation(size[:], theta[:], ACT.Abs)
-            turns = ring.tile([P, M], U32, name="turns")
-            nc.scalar.activation(turns[:], size[:], ACT.Copy, scale=1.0 / TWO_PI, bias=-0.25)
+            nc.scalar.activation(turns, size[:], ACT.Copy, scale=1.0 / TWO_PI, bias=-0.25)
             whole = ring.tile([P, M], F32, name="whole")
-            nc.scalar.activation(whole[:], turns[:], ACT.Copy, scale=-TWO_PI)
-            rest = psum.tile([P, M], F32, name="rest")
+            nc.scalar.activation(whole[:], turns, ACT.Copy, scale=-TWO_PI)
             add_turned(rest, size, whole)
             nc.scalar.activation(cosine[b][:, i, :], rest[:], ACT.Sin, scale=-1.0, bias=half_pi[:])
 
         def cos_by_vector(s, cols):
             b, i = divmod(s, PACK)
             width = cols.stop - cols.start
-            theta = ring.tile([P, width], F32, name="pitched")
-            nc.vector.scalar_tensor_tensor(theta[:], x[b][:, i, cols], pitch_sb[:, b, i:i + 1], slopes[s][:, cols],
+            turns, size = h[H_OF[s]][:, cols], sizes[(s + 1) % 2]
+            nc.vector.scalar_tensor_tensor(size[:, cols], x[b][:, i, cols], pitch_sb[:, b, i:i + 1], slopes[s][:, cols],
                                            ALU.mult, ALU.add)
-            size = ring.tile([P, width], F32, name="size")
-            nc.scalar.activation(size[:], theta[:], ACT.Abs)
-            turns = ring.tile([P, width], U32, name="turns")
-            nc.scalar.activation(turns[:], size[:], ACT.Copy, scale=1.0 / TWO_PI, bias=-0.25)
-            rest = ring.tile([P, width], F32, name="whole")
-            nc.vector.scalar_tensor_tensor(rest[:], turns[:].bitcast(I32), TWO_PI, size[:], ALU.mult, ALU.subtract)
+            nc.scalar.activation(size[:, cols], size[:, cols], ACT.Abs)
+            nc.scalar.activation(turns.bitcast(U32), size[:, cols], ACT.Copy, scale=1.0 / TWO_PI, bias=-0.25)
+            rest = ring.tile([P, width], F32, name="rest", bufs=3)
+            nc.vector.scalar_tensor_tensor(rest[:], turns.bitcast(I32), TWO_PI, size[:, cols], ALU.mult, ALU.subtract)
             nc.scalar.activation(cosine[b][:, i, cols], rest[:], ACT.Sin, bias=half_pi[:])
 
-        def quantise_z(b, cols, room):
-            z = room[:].bitcast(BF16)
+        def quantise_z(b, cols):
+            z = ring.tile([P, PACK * (cols.stop - cols.start)], BF16, name="z", align_bytes=64)[:]
             nc.vector.tensor_tensor(z.rearrange("p (c e i) -> p c i e", e=2, i=PACK),
                                     x[b][:, :, cols].rearrange("p i (c e) -> p c i e", e=2),
                                     cosine[b][:, :, cols].rearrange("p i (c e) -> p c i e", e=2), ALU.mult)
             nc.vector.quantize_mx(out=z_codes[b][:, cols].bitcast(E4M3), scales=z_sc[b][:, cols], in_=z)
 
-        halves = (slice(0, M // 2), slice(M // 2, M))
+        pieces = (slice(0, 128), slice(128, 256), slice(256, 384), slice(384, 512))
+        for a in range(2):
+            quantise_w1(a, 0, 0)
+        for s in range(2):
+            gained_feature(s)
+        for a in range(2):
+            quantise_w1(a, 0, 1)
         for s in range(8):
-            if s % 2 == 0:
-                for a in range(2):
-                    quantise_w1(a, s // 4, s % 4 // 2)
-            features(s)
+            larger_feature(s)
             put(s)
-            if s in (5, 6):
-                quantise_z(0, halves[s - 5], h_of[s])
-                quantise_w2(s - 5)
-            if s < 7:
-                pick(s, slice(0, M))
-                cos_by_tensor(s)
-        for cols in halves:
+            if s == 7:
+                break
+            pick(s, slice(0, M))
+            if s < 6:
+                gained_feature(s + 2)
+            cos_by_tensor(s)
+            if s in (0, 2):
+                for a in range(2):
+                    quantise_w1(a, 1, (0, 2).index(s))
+            if s == 3:
+                for cols in (slice(0, M // 2), slice(M // 2, M)):
+                    quantise_z(0, cols)
+            if s in (3, 4):
+                quantise_w2((3, 4).index(s))
+        for cols in pieces:
             pick(7, cols)
             cos_by_vector(7, cols)
 
-        for cols, banks in zip(halves, (("first", "second"), ("theta", "rest"))):
-            accs = [psum.tile([P, M // 2], F32, name=banks[n % 2]) for n in range(N // P)]
-            room = ring.tile([P, S], F32, name="h", bufs=3, align_bytes=64)
-            quantise_z(1, cols, room)
+        banks = ((turn_banks[2],), (turn_banks[3],), (turn_banks[1],), (turn_banks[0],))
+
+        def product(b, piece):
+            cols = pieces[piece]
+            width = cols.stop - cols.start
+            per_bank = M // width
             for n in range(N // P):
-                for b in range(2):
-                    nc.tensor.matmul_mx(out=accs[n][:], lhsT=w2_codes[b][:, n * P:(n + 1) * P].bitcast(E4M3),
-                                        lhsT_scale=w2_sc[b][:, n * P:(n + 1) * P],
-                                        rhs=z_codes[b][:, cols].bitcast(E4M3),
-                                        rhs_scale=z_sc[b][:, cols], start=(b == 0), stop=(b == 1))
-                result = keep([P, M // 2], F32, "result%d%d" % (n, cols.start))
-                if cols.start == 0 or n % 2 == 0:
-                    nc.scalar.copy(result[:], accs[n][:])
+                bank = banks[piece][n // per_bank]
+                nc.tensor.matmul_mx(out=bank[:, n % per_bank * width:(n % per_bank + 1) * width],
+                                    lhsT=w2_codes[b][:, n * P:(n + 1) * P].bitcast(E4M3),
+                                    lhsT_scale=w2_sc[b][:, n * P:(n + 1) * P],
+                                    rhs=z_codes[b][:, cols].bitcast(E4M3), rhs_scale=z_sc[b][:, cols],
+                                    start=(b == 0 and n % per_bank == 0), stop=(b == 1 and n % per_bank == per_bank - 1))
+
+        for piece in range(len(pieces)):
+            product(0, piece)
+        for piece, cols in enumerate(pieces):
+            quantise_z(1, cols)
+            product(1, piece)
+            per_bank = M // (cols.stop - cols.start)
+            for e, bank in enumerate(banks[piece]):
+                result = keep([P, M], F32, "result%d%d" % (piece, e))
+                if piece == 2:
+                    nc.vector.tensor_copy(result[:], bank[:])
                 else:
-                    nc.vector.tensor_copy(result[:], accs[n][:])
-                nc.sync.dma_start(out=out[n * P:(n + 1) * P, cols], in_=result[:])
+                    nc.scalar.copy(result[:], bank[:])
+                rows = out[per_bank * P * e:per_bank * P * (e + 1), cols]
+                nc.sync.dma_start(out=rows.rearrange("(n p) c -> p n c", p=P),
+                                  in_=result[:].rearrange("p (n c) -> p n c", n=per_bank))

@@ -15,11 +15,12 @@ ALU, ACT = mybir.AluOpType, mybir.ActivationFunctionType
 P = 128
 PACK = 4
 KP = P * PACK
+PASSES = 2
+SLICES = PASSES * PACK
+LAST = SLICES - 1
+QUADRANT = 32
+GROUP = 16
 TWO_PI = 2.0 * math.pi
-T_OF = (3, 2, 3, 2, 3, 2, 3)
-F_OF = (0, 1, 0, 1, 2, 3, 0, 1)
-TH_OF = (2, 3, 0, 1, 2, 3, 0)
-H_OF = (0, 0, 1, 0, 1, 0, 1, 0)
 
 
 def tile_list_blade_load_cells_kernel(tc, tab_words, tab_scales, offs, offs2, offs3, w1, w4_words, w4_scales,
@@ -34,101 +35,101 @@ def tile_list_blade_load_cells_kernel(tc, tab_words, tab_scales, offs, offs2, of
         def keep(shape, dtype, name):
             return held.tile(shape, dtype, name=name, align_bytes=64)
 
-        tab_sc = keep([P, 2 * T], U8, "tab_sc")
-        w4_sc_raw = keep([P, 2 * H], U8, "w4_sc_raw")
+        tab_sc = keep([P, PASSES * T], U8, "tab_sc")
+        w4_sc_raw = keep([P, PASSES * H], U8, "w4_sc_raw")
         nc.vector.memset(w4_sc_raw[:].bitcast(I32), 0)
         nc.vector.memset(tab_sc[:].bitcast(I32), 0)
-
-        def load_scales(queue, tile, rows):
-            for q in range(4):
-                queue.dma_start(
-                    out=tile[32 * q:32 * q + 4, :].bitcast(I32).rearrange("r (a c) -> r a c", a=2),
-                    in_=rows[:, 4 * q:4 * q + 4, :].bitcast(I32).rearrange("a r c -> r a c"))
-
-        gain_sb = keep([P, 2, PACK], F32, "gain_sb")
-        pitch_sb = keep([P, 2, PACK], F32, "pitch_sb")
+        gain_sb = keep([P, PASSES, PACK], F32, "gain_sb")
+        pitch_sb = keep([P, PASSES, PACK], F32, "pitch_sb")
         ident = keep([P, P], F32, "ident")
         make_identity(nc, ident[:])
         half_pi = keep([P, 1], F32, "half_pi")
         nc.vector.memset(half_pi[:], 1.0)
         nc.vector.tensor_scalar(half_pi[:], half_pi[:], math.pi / 2, None, ALU.mult)
 
-        list1 = held.tile([P, S // 16], U16, name="list1")
-        list2 = held.tile([P, S // 16], U16, name="list2")
-        list3 = held.tile([P, M // 16], U16, name="list3")
-        w4_raw = keep([P, 2, H // 2], I32, "w4_raw")
-        tab = [keep([P, T], I32, "tab%d" % a) for a in range(2)]
-        pages = [keep([P, T2], F32, "page%d" % s) for s in range(8)]
-        slopes = [keep([P, M], F32, "slope%d" % s) for s in range(8)]
+        list1 = held.tile([P, S // GROUP], U16, name="list1")
+        list2 = held.tile([P, S // GROUP], U16, name="list2")
+        list3 = held.tile([P, M // GROUP], U16, name="list3")
+        w4_raw = keep([P, PASSES, H // 2], I32, "w4_raw")
+        tab = [keep([P, T], I32, "tab%d" % a) for a in range(PASSES)]
+        pages = [keep([P, T2], F32, "page%d" % s) for s in range(SLICES)]
+        slopes = [keep([P, M], F32, "slope%d" % s) for s in range(SLICES)]
         wgs_first = keep([P, 1, S], F32, "wgs_first")
         wgs_rest = keep([P, PACK - 1, S], F32, "wgs_rest")
         wgs_sb = [wgs_first[:, 0, :]] + [wgs_rest[:, i, :] for i in range(PACK - 1)]
         wgt_sb = keep([P, M], F32, "wgt_sb")
-        page_rows = page0.rearrange("(b p i) c -> b i p c", b=2, i=PACK)
-        slope_rows = slope.rearrange("(b p i) c -> b i p c", b=2, i=PACK)
+        page_rows = page0.rearrange("(b p i) c -> b i p c", b=PASSES, i=PACK)
+        slope_rows = slope.rearrange("(b p i) c -> b i p c", b=PASSES, i=PACK)
         wgs_rows = wgs.rearrange("(q i) j -> q i j", i=PACK)
+        w1_raw, w2_raw = {}, {}
 
-        def load_rows(w, a, cols):
-            raw = raws.tile([P, PACK, 512], F32, name="raw")
-            nc.sync.dma_start(out=raw[:], in_=w[KP * a:KP * (a + 1), cols].rearrange("(p j) c -> p j c", j=PACK))
-            return raw
-
-        def load_wgs(tile, rows):
-            for q in range(4):
-                nc.sync.dma_start(out=tile[32 * q:32 * q + 32], in_=wgs_rows[:, rows, :])
-
-        def load_page(s):
-            nc.sync.dma_start(out=pages[s][:], in_=page_rows[s // 4, s % 4])
-
-        def load_slope(s):
-            nc.sync.dma_start(out=slopes[s][:], in_=slope_rows[s // 4, s % 4])
+        def load_scales(tile, rows):
+            for q in range(P // QUADRANT):
+                nc.sync.dma_start(
+                    out=tile[QUADRANT * q:QUADRANT * q + 4, :].bitcast(I32).rearrange("r (a c) -> r a c", a=PASSES),
+                    in_=rows[:, 4 * q:4 * q + 4, :].bitcast(I32).rearrange("a r c -> r a c"))
 
         def load_table(a):
             nc.sync.dma_start(out=tab[a][:], in_=tab_words[a].rearrange("p t i -> p (t i)").bitcast(I32))
 
+        def load_weight(w, g, first_col):
+            raw = raws.tile([P, PACK, KP], F32, name="raw")
+            rows = w[KP * g:KP * (g + 1), first_col:first_col + KP]
+            nc.sync.dma_start(out=raw[:], in_=rows.rearrange("(p j) c -> p j c", j=PACK))
+            return raw
+
+        def load_by_slice(tile, vector):
+            nc.sync.dma_start(out=tile[:], in_=vector.rearrange("(b p i) -> p b i", b=PASSES, i=PACK))
+
+        def load_wgs(tile, rows):
+            for q in range(P // QUADRANT):
+                nc.sync.dma_start(out=tile[QUADRANT * q:QUADRANT * (q + 1)], in_=wgs_rows[:, rows, :])
+
+        def load_page(s):
+            nc.sync.dma_start(out=pages[s][:], in_=page_rows[s // PACK, s % PACK])
+
+        def load_slope(s):
+            nc.sync.dma_start(out=slopes[s][:], in_=slope_rows[s // PACK, s % PACK])
+
         nc.sync.dma_start(out=w4_raw[:], in_=w4_words.bitcast(I32).rearrange("a p c -> p a c"))
-        load_scales(nc.sync, w4_sc_raw, w4_scales)
+        load_scales(w4_sc_raw, w4_scales)
         nc.sync.dma_start(list1[:], offs)
         load_table(0)
-        load_scales(nc.sync, tab_sc, tab_scales)
+        load_scales(tab_sc, tab_scales)
         load_table(1)
-        w1_raw = {}
-        for a in range(2):
-            w1_raw[a, 0] = load_rows(w1, a, slice(0, 512))
-        nc.sync.dma_start(out=gain_sb[:], in_=gain.rearrange("(b p i) -> p b i", b=2, i=PACK))
+        w1_raw[0, 0] = load_weight(w1, 0, 0)
+        load_by_slice(gain_sb, gain)
+        w1_raw[1, 0] = load_weight(w1, 1, 0)
         nc.sync.dma_start(list2[:], offs2)
         load_page(0)
         load_wgs(wgs_first, slice(0, 1))
         nc.sync.dma_start(list3[:], offs3)
         nc.sync.dma_start(out=wgt_sb[:], in_=wgt)
+        load_by_slice(pitch_sb, pitch)
+        load_slope(0)
         load_page(1)
         load_wgs(wgs_rest, slice(1, PACK))
-        nc.sync.dma_start(out=pitch_sb[:], in_=pitch.rearrange("(b p i) -> p b i", b=2, i=PACK))
-        w2_raw = {}
-        for s in range(2, 6):
-            load_slope(s - 2)
-            if s < 4:
-                w1_raw[s - 2, 1] = load_rows(w1, s - 2, slice(512, 1024))
-            else:
-                w2_raw[s - 4] = load_rows(w2, s - 4, slice(0, N))
+        for s in range(2, SLICES):
+            load_slope(s - 1)
+            if s < 2 + PASSES:
+                w1_raw[s - 2, 1] = load_weight(w1, s - 2, KP)
+            elif s < 2 + 2 * PASSES:
+                w2_raw[s - 2 - PASSES] = load_weight(w2, s - 2 - PASSES, 0)
             load_page(s)
-        for s in range(6, 8):
-            load_slope(2 * s - 8)
-            load_slope(2 * s - 7)
-            load_page(s)
+        load_slope(LAST)
 
-        w4_codes = keep([P, 2 * 2 * H], U8, "w4_codes")
-        w4_sc = keep([P, 2 * H], U8, "w4_sc")
+        w4_codes = keep([P, PASSES * 2 * H], U8, "w4_codes")
+        w4_sc = keep([P, PASSES * H], U8, "w4_sc")
         nc.vector.tensor_copy(
-            w4_codes[:].bitcast(U16).rearrange("p (g i m) -> p g i m", g=4, i=PACK),
-            w4_raw[:].rearrange("p a c -> p (a c)").bitcast(U16).rearrange("p (g m i) -> p g i m", g=4, i=PACK))
+            w4_codes[:].bitcast(U16).rearrange("p (g i m) -> p g i m", m=P, i=PACK),
+            w4_raw[:].rearrange("p a c -> p (a c)").bitcast(U16).rearrange("p (g m i) -> p g i m", m=P, i=PACK))
         nc.vector.tensor_copy(
-            w4_sc[:].rearrange("p (g i m) -> p g i m", g=4, i=PACK),
-            w4_sc_raw[:].rearrange("p (g m i) -> p g i m", g=4, i=PACK))
+            w4_sc[:].rearrange("p (g i m) -> p g i m", m=P, i=PACK),
+            w4_sc_raw[:].rearrange("p (g m i) -> p g i m", m=P, i=PACK))
 
-        v_codes = [keep([P, S], U32, "v_codes%d" % a) for a in range(2)]
-        v_sc = [keep([P, S], U8, "v_sc%d" % a) for a in range(2)]
-        for a in range(2):
+        v_codes = [keep([P, S], U32, "v_codes%d" % a) for a in range(PASSES)]
+        v_sc = [keep([P, S], U8, "v_sc%d" % a) for a in range(PASSES)]
+        for a in range(PASSES):
             nc.vector.tensor_copy(v_sc[a][:], tab_sc[:, T * a:T * (a + 1)].indirect(list1[:]))
             nc.vector.tensor_copy(v_codes[a][:], tab[a][:].bitcast(U32).indirect(list1[:]))
 
@@ -136,19 +137,19 @@ def tile_list_blade_load_cells_kernel(tc, tab_words, tab_scales, offs, offs2, of
 
         def quantise_w1(a, b, u):
             grouped = ring.tile([P, 2, P, PACK], BF16, name="w1_bf", bufs=4, align_bytes=64)
-            dst = grouped[:].rearrange("p i m j -> p m j i")
+            dst = grouped[:].rearrange("p e m j -> p m j e")
             src = w1_raw[a, b][:].rearrange("p j (m i) -> p m j i", i=PACK)[:, :, :, 2 * u:2 * u + 2]
-            if (a, b, u) == (1, 0, 0):
+            if (a, b, u) == (PASSES - 1, 0, 0):
                 nc.vector.tensor_copy(dst, src)
             else:
                 nc.scalar.copy(dst, src)
             w1_codes[a, b, u] = keep([P, 2 * P], U32, "w1_codes%d%d%d" % (a, b, u))
             w1_sc[a, b, u] = keep([P, 2 * P], U8, "w1_sc%d%d%d" % (a, b, u))
             nc.vector.quantize_mx(out=w1_codes[a, b, u][:].bitcast(E4M3), scales=w1_sc[a, b, u][:],
-                                  in_=grouped[:].rearrange("p i m j -> p (i m j)"))
+                                  in_=grouped[:].rearrange("p e m j -> p (e m j)"))
 
-        w2_codes = [keep([P, N], U32, "w2_codes%d" % b) for b in range(2)]
-        w2_sc = [keep([P, N], U8, "w2_sc%d" % b) for b in range(2)]
+        w2_codes = [keep([P, N], U32, "w2_codes%d" % b) for b in range(PASSES)]
+        w2_sc = [keep([P, N], U8, "w2_sc%d" % b) for b in range(PASSES)]
 
         def quantise_w2(b):
             grouped = keep([P, N, PACK], BF16, "w2_bf%d" % b)
@@ -158,138 +159,134 @@ def tile_list_blade_load_cells_kernel(tc, tab_words, tab_scales, offs, offs2, of
             nc.vector.quantize_mx(out=w2_codes[b][:].bitcast(E4M3), scales=w2_sc[b][:],
                                   in_=grouped[:].rearrange("p c j -> p (c j)"))
 
-        x = [keep([P, PACK, M], F32, "x%d" % b) for b in range(2)]
-        cosine = [keep([P, PACK, M], F32, "cosine%d" % b) for b in range(2)]
-        z_codes = [keep([P, M], U32, "z_codes%d" % b) for b in range(2)]
-        z_sc = [keep([P, M], U8, "z_sc%d" % b) for b in range(2)]
+        x = [keep([P, PACK, M], F32, "x%d" % b) for b in range(PASSES)]
+        cosine = [keep([P, PACK, M], F32, "cosine%d" % b) for b in range(PASSES)]
+        z_codes = [keep([P, M], U32, "z_codes%d" % b) for b in range(PASSES)]
+        z_sc = [keep([P, M], U8, "z_sc%d" % b) for b in range(PASSES)]
         gained = {}
-        h = [keep([P, S], F32, "h%d" % e) for e in range(4)]
+        h = [keep([P, S], F32, "h%d" % e) for e in range(2)]
+        turn_counts = [keep([P, M], F32, "turns%d" % e) for e in range(2)]
         sizes = [keep([P, M], F32, "size%d" % e) for e in range(2)]
-        turn_banks = [psum.tile([P, M], F32, name="turn%d" % e) for e in range(4)]
+        angle_banks = [psum.tile([P, M], F32, name="angle%d" % e) for e in range(2)]
+        feature_banks = [psum.tile([P, S], F32, name="feature%d" % e) for e in range(2)]
         rest_banks = [psum.tile([P, M], F32, name="rest%d" % e) for e in range(2)]
 
         def gained_feature(s):
             b, i = divmod(s, PACK)
-            second = psum.tile([P, S], F32, name="second", bufs=2)
-            for a in range(2):
-                col = (2 * a + b) * KP + i * P
-                nc.tensor.matmul_mx(out=second[:], lhsT=w4_codes[:, 2 * col:2 * (col + P)].bitcast(E2M1),
+            bank = feature_banks[s % 2]
+            for a in range(PASSES):
+                col = (PASSES * a + b) * KP + i * P
+                nc.tensor.matmul_mx(out=bank[:], lhsT=w4_codes[:, 2 * col:2 * (col + P)].bitcast(E2M1),
                                     lhsT_scale=w4_sc[:, col:col + P], rhs=v_codes[a][:].bitcast(E4M3),
-                                    rhs_scale=v_sc[a][:], start=(a == 0), stop=(a == 1))
+                                    rhs_scale=v_sc[a][:], start=(a == 0), stop=(a == PASSES - 1))
             gained[s] = ring.tile([P, S], F32, name="gained")
-            nc.scalar.activation(gained[s][:], second[:], ACT.Copy, scale=gain_sb[:, b, i:i + 1])
+            nc.scalar.activation(gained[s][:], bank[:], ACT.Copy, scale=gain_sb[:, b, i:i + 1])
 
         def larger_feature(s):
             b, i = divmod(s, PACK)
             u, e = divmod(i, 2)
-            first = turn_banks[F_OF[s]]
-            for a in range(2):
-                nc.tensor.matmul_mx(out=first[:], lhsT=w1_codes[a, b, u][:, e * P:(e + 1) * P].bitcast(E4M3),
+            bank = feature_banks[s % 2]
+            for a in range(PASSES):
+                nc.tensor.matmul_mx(out=bank[:], lhsT=w1_codes[a, b, u][:, e * P:(e + 1) * P].bitcast(E4M3),
                                     lhsT_scale=w1_sc[a, b, u][:, e * P:(e + 1) * P], rhs=v_codes[a][:].bitcast(E4M3),
-                                    rhs_scale=v_sc[a][:], start=(a == 0), stop=(a == 1))
-            nc.vector.tensor_tensor(h[H_OF[s]][:], first[:], gained[s][:], ALU.max)
+                                    rhs_scale=v_sc[a][:], start=(a == 0), stop=(a == PASSES - 1))
+            nc.vector.tensor_tensor(h[s % 2][:], bank[:], gained[s][:], ALU.max)
 
         def put(s):
-            i = s % PACK
-            nc.vector.tensor_tensor(pages[s][:].indirect(list2[:]), h[H_OF[s]][:], wgs_sb[i], ALU.mult)
+            nc.vector.tensor_tensor(pages[s][:].indirect(list2[:]), h[s % 2][:], wgs_sb[s % PACK], ALU.mult)
 
         def pick(s, cols):
             b, i = divmod(s, PACK)
-            nc.vector.tensor_tensor(x[b][:, i, cols], pages[s][:].indirect(list3[:, cols.start // 16:cols.stop // 16]),
-                                    wgt_sb[:, cols], ALU.mult)
+            entries = list3[:, cols.start // GROUP:cols.stop // GROUP]
+            nc.vector.tensor_tensor(x[b][:, i, cols], pages[s][:].indirect(entries), wgt_sb[:, cols], ALU.mult)
 
-        def add_turned(bank, one, other):
+        def add_transposed(bank, one, other):
+            blocks = M // P
             for n, src in enumerate((one, other)):
-                for c in range(4):
+                for c in range(blocks):
                     nc.tensor.matmul(bank[:, c * P:(c + 1) * P], lhsT=src[:, c * P:(c + 1) * P], rhs=ident[:],
-                                     is_transpose=True, start=(n == 0 and c == 0), stop=(n == 1 and c == 3))
+                                     is_transpose=True, start=(n == 0 and c == 0), stop=(n == 1 and c == blocks - 1))
 
-        def cos_by_tensor(s):
+        def cosine_by_tensor(s):
             b, i = divmod(s, PACK)
-            theta, rest, size = turn_banks[TH_OF[s]], rest_banks[s % 2], sizes[s % 2]
-            turns = h[T_OF[s]][:].bitcast(U32)
+            angle, rest, size = angle_banks[s % 2], rest_banks[s % 2], sizes[s % 2]
+            turns = turn_counts[s % 2][:].bitcast(U32)
             nc.scalar.activation(size[:], x[b][:, i, :], ACT.Copy, scale=pitch_sb[:, b, i:i + 1])
-            add_turned(theta, slopes[s], size)
-            nc.scalar.activation(size[:], theta[:], ACT.Abs)
+            add_transposed(angle, slopes[s], size)
+            nc.scalar.activation(size[:], angle[:], ACT.Abs)
             nc.scalar.activation(turns, size[:], ACT.Copy, scale=1.0 / TWO_PI, bias=-0.25)
             whole = ring.tile([P, M], F32, name="whole")
             nc.scalar.activation(whole[:], turns, ACT.Copy, scale=-TWO_PI)
-            add_turned(rest, size, whole)
+            add_transposed(rest, size, whole)
             nc.scalar.activation(cosine[b][:, i, :], rest[:], ACT.Sin, scale=-1.0, bias=half_pi[:])
 
-        def cos_by_vector(s, cols):
+        def cosine_by_vector(s, cols):
             b, i = divmod(s, PACK)
-            width = cols.stop - cols.start
-            turns, size = h[H_OF[s]][:, cols], sizes[(s + 1) % 2]
-            nc.vector.scalar_tensor_tensor(size[:, cols], x[b][:, i, cols], pitch_sb[:, b, i:i + 1], slopes[s][:, cols],
+            angle, turns = sizes[(s - 1) % 2][:, cols], h[s % 2][:, cols].bitcast(I32)
+            nc.vector.scalar_tensor_tensor(angle, x[b][:, i, cols], pitch_sb[:, b, i:i + 1], slopes[s][:, cols],
                                            ALU.mult, ALU.add)
-            nc.scalar.activation(size[:, cols], size[:, cols], ACT.Abs)
-            nc.scalar.activation(turns.bitcast(U32), size[:, cols], ACT.Copy, scale=1.0 / TWO_PI, bias=-0.25)
-            rest = ring.tile([P, width], F32, name="rest", bufs=3)
-            nc.vector.scalar_tensor_tensor(rest[:], turns.bitcast(I32), TWO_PI, size[:, cols], ALU.mult, ALU.subtract)
-            nc.scalar.activation(cosine[b][:, i, cols], rest[:], ACT.Sin, bias=half_pi[:])
+            nc.vector.tensor_scalar(turns, angle, 1.0 / TWO_PI, -0.25, ALU.mult, ALU.add)
+            minus_rest = ring.tile([P, P], F32, name="minus_rest", bufs=M // P)
+            nc.vector.scalar_tensor_tensor(minus_rest[:], turns, TWO_PI, angle, ALU.mult, ALU.subtract)
+            nc.scalar.activation(cosine[b][:, i, cols], minus_rest[:], ACT.Sin, bias=half_pi[:])
 
         def quantise_z(b, cols):
-            z = ring.tile([P, PACK * (cols.stop - cols.start)], BF16, name="z", align_bytes=64)[:]
+            z = ring.tile([P, PACK * (cols.stop - cols.start)], BF16, name="z", bufs=3, align_bytes=64)[:]
             nc.vector.tensor_tensor(z.rearrange("p (c e i) -> p c i e", e=2, i=PACK),
                                     x[b][:, :, cols].rearrange("p i (c e) -> p c i e", e=2),
                                     cosine[b][:, :, cols].rearrange("p i (c e) -> p c i e", e=2), ALU.mult)
             nc.vector.quantize_mx(out=z_codes[b][:, cols].bitcast(E4M3), scales=z_sc[b][:, cols], in_=z)
 
-        pieces = (slice(0, 128), slice(128, 256), slice(256, 384), slice(384, 512))
-        for a in range(2):
+        for a in range(PASSES):
             quantise_w1(a, 0, 0)
         for s in range(2):
             gained_feature(s)
-        for a in range(2):
+        for a in range(PASSES):
             quantise_w1(a, 0, 1)
-        for s in range(8):
+        for s in range(LAST):
             larger_feature(s)
             put(s)
-            if s == 7:
-                break
             pick(s, slice(0, M))
-            if s < 6:
+            if s + 2 < SLICES:
                 gained_feature(s + 2)
-            cos_by_tensor(s)
-            if s in (0, 2):
-                for a in range(2):
-                    quantise_w1(a, 1, (0, 2).index(s))
-            if s == 3:
+            cosine_by_tensor(s)
+            if s < PACK and s % 2 == 0:
+                for a in range(PASSES):
+                    quantise_w1(a, 1, s // 2)
+            if s == PACK - 1:
                 for cols in (slice(0, M // 2), slice(M // 2, M)):
                     quantise_z(0, cols)
-            if s in (3, 4):
-                quantise_w2((3, 4).index(s))
-        for cols in pieces:
-            pick(7, cols)
-            cos_by_vector(7, cols)
+            if 0 <= s - (PACK - 1) < PASSES:
+                quantise_w2(s - (PACK - 1))
 
-        banks = ((turn_banks[2],), (turn_banks[3],), (turn_banks[1],), (turn_banks[0],))
+        pieces = [slice(c, c + P) for c in range(0, M, P)]
+        larger_feature(LAST)
+        put(LAST)
+        for cols in pieces:
+            pick(LAST, cols)
+            cosine_by_vector(LAST, cols)
+
+        out_banks = (feature_banks[0], feature_banks[1], angle_banks[1], angle_banks[0])
+        blocks = N // P
 
         def product(b, piece):
             cols = pieces[piece]
-            width = cols.stop - cols.start
-            per_bank = M // width
-            for n in range(N // P):
-                bank = banks[piece][n // per_bank]
-                nc.tensor.matmul_mx(out=bank[:, n % per_bank * width:(n % per_bank + 1) * width],
+            for n in range(blocks):
+                nc.tensor.matmul_mx(out=out_banks[piece][:, n * P:(n + 1) * P],
                                     lhsT=w2_codes[b][:, n * P:(n + 1) * P].bitcast(E4M3),
                                     lhsT_scale=w2_sc[b][:, n * P:(n + 1) * P],
                                     rhs=z_codes[b][:, cols].bitcast(E4M3), rhs_scale=z_sc[b][:, cols],
-                                    start=(b == 0 and n % per_bank == 0), stop=(b == 1 and n % per_bank == per_bank - 1))
+                                    start=(b == 0 and n == 0), stop=(b == PASSES - 1 and n == blocks - 1))
 
         for piece in range(len(pieces)):
             product(0, piece)
         for piece, cols in enumerate(pieces):
             quantise_z(1, cols)
             product(1, piece)
-            per_bank = M // (cols.stop - cols.start)
-            for e, bank in enumerate(banks[piece]):
-                result = keep([P, M], F32, "result%d%d" % (piece, e))
-                if piece == 2:
-                    nc.vector.tensor_copy(result[:], bank[:])
-                else:
-                    nc.scalar.copy(result[:], bank[:])
-                rows = out[per_bank * P * e:per_bank * P * (e + 1), cols]
-                nc.sync.dma_start(out=rows.rearrange("(n p) c -> p n c", p=P),
-                                  in_=result[:].rearrange("p (n c) -> p n c", n=per_bank))
+            result = keep([P, blocks, P], F32, "result%d" % piece)
+            sums = out_banks[piece][:].rearrange("p (n c) -> p n c", n=blocks)
+            if piece == len(pieces) - 2:
+                nc.vector.tensor_copy(result[:], sums)
+            else:
+                nc.scalar.copy(result[:], sums)
+            nc.sync.dma_start(out=out[:, cols].rearrange("(n p) c -> p n c", p=P), in_=result[:])

import math
from contextlib import ExitStack

import concourse.mybir as mybir
from concourse.masks import make_identity

K, T, S, H, T2, M, N = 1024, 2048, 512, 1024, 1024, 512, 512
FLOPS = 2 * (2 * K * H * S + H * N * M)

F32, BF16 = mybir.dt.float32, mybir.dt.bfloat16
I32, U32, U16, U8 = mybir.dt.int32, mybir.dt.uint32, mybir.dt.uint16, mybir.dt.uint8
E4M3, E2M1 = mybir.dt.float8_e4m3fn_x4, mybir.dt.float4_e2m1fn_x4
ALU, ACT = mybir.AluOpType, mybir.ActivationFunctionType

P = 128
PACK = 4
KP = P * PACK
PASSES = 2
SLICES = PASSES * PACK
LAST = SLICES - 1
QUADRANT = 32
GROUP = 16
TWO_PI = 2.0 * math.pi


def tile_list_blade_load_cells_kernel(tc, tab_words, tab_scales, offs, offs2, offs3, w1, w4_words, w4_scales,
                                                gain, wgs, page0, wgt, pitch, slope, w2, out):
    nc = tc.nc
    with ExitStack() as ctx:
        held = ctx.enter_context(tc.tile_pool(name="held", bufs=1))
        raws = ctx.enter_context(tc.tile_pool(name="raws", bufs=4))
        ring = ctx.enter_context(tc.tile_pool(name="ring", bufs=2))
        psum = ctx.enter_context(tc.psum_pool(name="psum", bufs=1))

        def keep(shape, dtype, name):
            return held.tile(shape, dtype, name=name, align_bytes=64)

        tab_sc = keep([P, PASSES * T], U8, "tab_sc")
        w4_sc_raw = keep([P, PASSES * H], U8, "w4_sc_raw")
        nc.vector.memset(w4_sc_raw[:].bitcast(I32), 0)
        nc.vector.memset(tab_sc[:].bitcast(I32), 0)
        gain_sb = keep([P, PASSES, PACK], F32, "gain_sb")
        pitch_sb = keep([P, PASSES, PACK], F32, "pitch_sb")
        ident = keep([P, P], F32, "ident")
        make_identity(nc, ident[:])
        half_pi = keep([P, 1], F32, "half_pi")
        nc.vector.memset(half_pi[:], 1.0)
        nc.vector.tensor_scalar(half_pi[:], half_pi[:], math.pi / 2, None, ALU.mult)

        list1 = held.tile([P, S // GROUP], U16, name="list1")
        list2 = held.tile([P, S // GROUP], U16, name="list2")
        list3 = held.tile([P, M // GROUP], U16, name="list3")
        w4_raw = keep([P, PASSES, H // 2], I32, "w4_raw")
        tab = [keep([P, T], I32, "tab%d" % a) for a in range(PASSES)]
        pages = [keep([P, T2], F32, "page%d" % s) for s in range(SLICES)]
        slopes = [keep([P, M], F32, "slope%d" % s) for s in range(SLICES)]
        wgs_first = keep([P, 1, S], F32, "wgs_first")
        wgs_rest = keep([P, PACK - 1, S], F32, "wgs_rest")
        wgs_sb = [wgs_first[:, 0, :]] + [wgs_rest[:, i, :] for i in range(PACK - 1)]
        wgt_sb = keep([P, M], F32, "wgt_sb")
        page_rows = page0.rearrange("(b p i) c -> b i p c", b=PASSES, i=PACK)
        slope_rows = slope.rearrange("(b p i) c -> b i p c", b=PASSES, i=PACK)
        wgs_rows = wgs.rearrange("(q i) j -> q i j", i=PACK)
        w1_raw, w2_raw = {}, {}

        def load_scales(tile, rows):
            for q in range(P // QUADRANT):
                nc.sync.dma_start(
                    out=tile[QUADRANT * q:QUADRANT * q + 4, :].bitcast(I32).rearrange("r (a c) -> r a c", a=PASSES),
                    in_=rows[:, 4 * q:4 * q + 4, :].bitcast(I32).rearrange("a r c -> r a c"))

        def load_table(a):
            nc.sync.dma_start(out=tab[a][:], in_=tab_words[a].rearrange("p t i -> p (t i)").bitcast(I32))

        def load_weight(w, g, first_col):
            raw = raws.tile([P, PACK, KP], F32, name="raw")
            rows = w[KP * g:KP * (g + 1), first_col:first_col + KP]
            nc.sync.dma_start(out=raw[:], in_=rows.rearrange("(p j) c -> p j c", j=PACK))
            return raw

        def load_by_slice(tile, vector):
            nc.sync.dma_start(out=tile[:], in_=vector.rearrange("(b p i) -> p b i", b=PASSES, i=PACK))

        def load_wgs(tile, rows):
            for q in range(P // QUADRANT):
                nc.sync.dma_start(out=tile[QUADRANT * q:QUADRANT * (q + 1)], in_=wgs_rows[:, rows, :])

        def load_page(s):
            nc.sync.dma_start(out=pages[s][:], in_=page_rows[s // PACK, s % PACK])

        def load_slope(s):
            nc.sync.dma_start(out=slopes[s][:], in_=slope_rows[s // PACK, s % PACK])

        nc.sync.dma_start(out=w4_raw[:], in_=w4_words.bitcast(I32).rearrange("a p c -> p a c"))
        load_scales(w4_sc_raw, w4_scales)
        nc.sync.dma_start(list1[:], offs)
        load_table(0)
        load_scales(tab_sc, tab_scales)
        load_table(1)
        w1_raw[0, 0] = load_weight(w1, 0, 0)
        load_by_slice(gain_sb, gain)
        w1_raw[1, 0] = load_weight(w1, 1, 0)
        nc.sync.dma_start(list2[:], offs2)
        load_page(0)
        load_wgs(wgs_first, slice(0, 1))
        nc.sync.dma_start(list3[:], offs3)
        nc.sync.dma_start(out=wgt_sb[:], in_=wgt)
        load_by_slice(pitch_sb, pitch)
        load_slope(0)
        load_page(1)
        load_wgs(wgs_rest, slice(1, PACK))
        for s in range(2, SLICES):
            load_slope(s - 1)
            if s < 2 + PASSES:
                w1_raw[s - 2, 1] = load_weight(w1, s - 2, KP)
            elif s < 2 + 2 * PASSES:
                w2_raw[s - 2 - PASSES] = load_weight(w2, s - 2 - PASSES, 0)
            load_page(s)
        load_slope(LAST)

        w4_codes = keep([P, PASSES * 2 * H], U8, "w4_codes")
        w4_sc = keep([P, PASSES * H], U8, "w4_sc")
        nc.vector.tensor_copy(
            w4_codes[:].bitcast(U16).rearrange("p (g i m) -> p g i m", m=P, i=PACK),
            w4_raw[:].rearrange("p a c -> p (a c)").bitcast(U16).rearrange("p (g m i) -> p g i m", m=P, i=PACK))
        nc.vector.tensor_copy(
            w4_sc[:].rearrange("p (g i m) -> p g i m", m=P, i=PACK),
            w4_sc_raw[:].rearrange("p (g m i) -> p g i m", m=P, i=PACK))

        v_codes = [keep([P, S], U32, "v_codes%d" % a) for a in range(PASSES)]
        v_sc = [keep([P, S], U8, "v_sc%d" % a) for a in range(PASSES)]
        for a in range(PASSES):
            nc.vector.tensor_copy(v_sc[a][:], tab_sc[:, T * a:T * (a + 1)].indirect(list1[:]))
            nc.vector.tensor_copy(v_codes[a][:], tab[a][:].bitcast(U32).indirect(list1[:]))

        w1_codes, w1_sc = {}, {}

        def quantise_w1(a, b, u):
            grouped = ring.tile([P, 2, P, PACK], BF16, name="w1_bf", bufs=4, align_bytes=64)
            dst = grouped[:].rearrange("p e m j -> p m j e")
            src = w1_raw[a, b][:].rearrange("p j (m i) -> p m j i", i=PACK)[:, :, :, 2 * u:2 * u + 2]
            if (a, b, u) == (PASSES - 1, 0, 0):
                nc.vector.tensor_copy(dst, src)
            else:
                nc.scalar.copy(dst, src)
            w1_codes[a, b, u] = keep([P, 2 * P], U32, "w1_codes%d%d%d" % (a, b, u))
            w1_sc[a, b, u] = keep([P, 2 * P], U8, "w1_sc%d%d%d" % (a, b, u))
            nc.vector.quantize_mx(out=w1_codes[a, b, u][:].bitcast(E4M3), scales=w1_sc[a, b, u][:],
                                  in_=grouped[:].rearrange("p e m j -> p (e m j)"))

        w2_codes = [keep([P, N], U32, "w2_codes%d" % b) for b in range(PASSES)]
        w2_sc = [keep([P, N], U8, "w2_sc%d" % b) for b in range(PASSES)]

        def quantise_w2(b):
            grouped = keep([P, N, PACK], BF16, "w2_bf%d" % b)
            for cols in (slice(0, N // 2), slice(N // 2, N)):
                nc.scalar.copy(grouped[:, cols, :].rearrange("p (c e) j -> p c j e", e=2),
                               w2_raw[b][:, :, cols].rearrange("p j (c e) -> p c j e", e=2))
            nc.vector.quantize_mx(out=w2_codes[b][:].bitcast(E4M3), scales=w2_sc[b][:],
                                  in_=grouped[:].rearrange("p c j -> p (c j)"))

        x = [keep([P, PACK, M], F32, "x%d" % b) for b in range(PASSES)]
        cosine = [keep([P, PACK, M], F32, "cosine%d" % b) for b in range(PASSES)]
        z_codes = [keep([P, M], U32, "z_codes%d" % b) for b in range(PASSES)]
        z_sc = [keep([P, M], U8, "z_sc%d" % b) for b in range(PASSES)]
        gained = {}
        h = [keep([P, S], F32, "h%d" % e) for e in range(2)]
        turn_counts = [keep([P, M], F32, "turns%d" % e) for e in range(2)]
        sizes = [keep([P, M], F32, "size%d" % e) for e in range(2)]
        angle_banks = [psum.tile([P, M], F32, name="angle%d" % e) for e in range(2)]
        feature_banks = [psum.tile([P, S], F32, name="feature%d" % e) for e in range(2)]
        rest_banks = [psum.tile([P, M], F32, name="rest%d" % e) for e in range(2)]

        def gained_feature(s):
            b, i = divmod(s, PACK)
            bank = feature_banks[s % 2]
            for a in range(PASSES):
                col = (PASSES * a + b) * KP + i * P
                nc.tensor.matmul_mx(out=bank[:], lhsT=w4_codes[:, 2 * col:2 * (col + P)].bitcast(E2M1),
                                    lhsT_scale=w4_sc[:, col:col + P], rhs=v_codes[a][:].bitcast(E4M3),
                                    rhs_scale=v_sc[a][:], start=(a == 0), stop=(a == PASSES - 1))
            gained[s] = ring.tile([P, S], F32, name="gained")
            nc.scalar.activation(gained[s][:], bank[:], ACT.Copy, scale=gain_sb[:, b, i:i + 1])

        def larger_feature(s):
            b, i = divmod(s, PACK)
            u, e = divmod(i, 2)
            bank = feature_banks[s % 2]
            for a in range(PASSES):
                nc.tensor.matmul_mx(out=bank[:], lhsT=w1_codes[a, b, u][:, e * P:(e + 1) * P].bitcast(E4M3),
                                    lhsT_scale=w1_sc[a, b, u][:, e * P:(e + 1) * P], rhs=v_codes[a][:].bitcast(E4M3),
                                    rhs_scale=v_sc[a][:], start=(a == 0), stop=(a == PASSES - 1))
            nc.vector.tensor_tensor(h[s % 2][:], bank[:], gained[s][:], ALU.max)

        def put(s):
            nc.vector.tensor_tensor(pages[s][:].indirect(list2[:]), h[s % 2][:], wgs_sb[s % PACK], ALU.mult)

        def pick(s, cols):
            b, i = divmod(s, PACK)
            entries = list3[:, cols.start // GROUP:cols.stop // GROUP]
            nc.vector.tensor_tensor(x[b][:, i, cols], pages[s][:].indirect(entries), wgt_sb[:, cols], ALU.mult)

        def add_transposed(bank, one, other):
            blocks = M // P
            for n, src in enumerate((one, other)):
                for c in range(blocks):
                    nc.tensor.matmul(bank[:, c * P:(c + 1) * P], lhsT=src[:, c * P:(c + 1) * P], rhs=ident[:],
                                     is_transpose=True, start=(n == 0 and c == 0), stop=(n == 1 and c == blocks - 1))

        def cosine_by_tensor(s):
            b, i = divmod(s, PACK)
            angle, rest, size = angle_banks[s % 2], rest_banks[s % 2], sizes[s % 2]
            turns = turn_counts[s % 2][:].bitcast(U32)
            nc.scalar.activation(size[:], x[b][:, i, :], ACT.Copy, scale=pitch_sb[:, b, i:i + 1])
            add_transposed(angle, slopes[s], size)
            nc.scalar.activation(size[:], angle[:], ACT.Abs)
            nc.scalar.activation(turns, size[:], ACT.Copy, scale=1.0 / TWO_PI, bias=-0.25)
            whole = ring.tile([P, M], F32, name="whole")
            nc.scalar.activation(whole[:], turns, ACT.Copy, scale=-TWO_PI)
            add_transposed(rest, size, whole)
            nc.scalar.activation(cosine[b][:, i, :], rest[:], ACT.Sin, scale=-1.0, bias=half_pi[:])

        def cosine_by_vector(s, cols):
            b, i = divmod(s, PACK)
            angle, turns = sizes[(s - 1) % 2][:, cols], h[s % 2][:, cols].bitcast(I32)
            nc.vector.scalar_tensor_tensor(angle, x[b][:, i, cols], pitch_sb[:, b, i:i + 1], slopes[s][:, cols],
                                           ALU.mult, ALU.add)
            nc.vector.tensor_scalar(turns, angle, 1.0 / TWO_PI, -0.25, ALU.mult, ALU.add)
            minus_rest = ring.tile([P, P], F32, name="minus_rest", bufs=M // P)
            nc.vector.scalar_tensor_tensor(minus_rest[:], turns, TWO_PI, angle, ALU.mult, ALU.subtract)
            nc.scalar.activation(cosine[b][:, i, cols], minus_rest[:], ACT.Sin, bias=half_pi[:])

        def quantise_z(b, cols):
            z = ring.tile([P, PACK * (cols.stop - cols.start)], BF16, name="z", bufs=3, align_bytes=64)[:]
            nc.vector.tensor_tensor(z.rearrange("p (c e i) -> p c i e", e=2, i=PACK),
                                    x[b][:, :, cols].rearrange("p i (c e) -> p c i e", e=2),
                                    cosine[b][:, :, cols].rearrange("p i (c e) -> p c i e", e=2), ALU.mult)
            nc.vector.quantize_mx(out=z_codes[b][:, cols].bitcast(E4M3), scales=z_sc[b][:, cols], in_=z)

        for a in range(PASSES):
            quantise_w1(a, 0, 0)
        for s in range(2):
            gained_feature(s)
        for a in range(PASSES):
            quantise_w1(a, 0, 1)
        for s in range(LAST):
            larger_feature(s)
            put(s)
            pick(s, slice(0, M))
            if s + 2 < SLICES:
                gained_feature(s + 2)
            cosine_by_tensor(s)
            if s < PACK and s % 2 == 0:
                for a in range(PASSES):
                    quantise_w1(a, 1, s // 2)
            if s == PACK - 1:
                for cols in (slice(0, M // 2), slice(M // 2, M)):
                    quantise_z(0, cols)
            if 0 <= s - (PACK - 1) < PASSES:
                quantise_w2(s - (PACK - 1))

        pieces = [slice(c, c + P) for c in range(0, M, P)]
        larger_feature(LAST)
        put(LAST)
        for cols in pieces:
            pick(LAST, cols)
            cosine_by_vector(LAST, cols)

        out_banks = (feature_banks[0], feature_banks[1], angle_banks[1], angle_banks[0])
        blocks = N // P

        def product(b, piece):
            cols = pieces[piece]
            for n in range(blocks):
                nc.tensor.matmul_mx(out=out_banks[piece][:, n * P:(n + 1) * P],
                                    lhsT=w2_codes[b][:, n * P:(n + 1) * P].bitcast(E4M3),
                                    lhsT_scale=w2_sc[b][:, n * P:(n + 1) * P],
                                    rhs=z_codes[b][:, cols].bitcast(E4M3), rhs_scale=z_sc[b][:, cols],
                                    start=(b == 0 and n == 0), stop=(b == PASSES - 1 and n == blocks - 1))

        for piece in range(len(pieces)):
            product(0, piece)
        for piece, cols in enumerate(pieces):
            quantise_z(1, cols)
            product(1, piece)
            result = keep([P, blocks, P], F32, "result%d" % piece)
            sums = out_banks[piece][:].rearrange("p (n c) -> p n c", n=blocks)
            if piece == len(pieces) - 2:
                nc.vector.tensor_copy(result[:], sums)
            else:
                nc.scalar.copy(result[:], sums)
            nc.sync.dma_start(out=out[:, cols].rearrange("(n p) c -> p n c", p=P), in_=result[:])
